import numpy as np
import ml_dtypes


def mxq(x, axis, fmt="e4m3"):
    dtype, down = {"e4m3": (ml_dtypes.float8_e4m3fn, 7), "e5m2": (ml_dtypes.float8_e5m2, 14)}[fmt]
    v = np.moveaxis(np.asarray(x, np.float32).astype(ml_dtypes.bfloat16).astype(np.float64), axis, -1)
    blocks = v.reshape(v.shape[:-1] + (-1, 32))
    amax = np.abs(blocks).max(-1, keepdims=True)
    byte = np.maximum(np.where(amax > 0, np.frexp(amax)[1] - 1 + 127, 0) - down, 1)
    scale = np.exp2(byte - 127.0)
    codes = (blocks / scale).astype(np.float32).astype(dtype).astype(np.float64)
    return np.moveaxis((codes * scale).reshape(v.shape), -1, axis)


WIDE = False


def mx_kscale(k):
    if not WIDE:
        return np.ones(k)
    levels = np.array([10, -10, 5, -5, 0])
    if k % 512:
        return np.exp2(np.random.permutation(np.resize(levels, k // 32))).repeat(32)
    a = np.empty((k // 512, 16))
    for p in range(k // 512):
        a[p, :8] = np.random.permutation(np.resize(levels, 8))
        for g in range(8):
            far = levels[np.abs(levels - a[p, g]) >= 10]
            a[p, g + 8] = far[np.random.randint(len(far))]
    return np.exp2(a.ravel()).repeat(32)


def f64(x):
    return np.asarray(x).astype(np.float64)


def striped(idx):
    return np.tile(idx.reshape(-1, 16).T, (8, 1)).astype(np.uint16)


def unstriped(offs):
    return offs[:16].T.reshape(-1).astype(np.int64)


def pack_weight(w):
    k, n = w.shape
    w = f64(np.asarray(w, np.float32).astype(ml_dtypes.bfloat16)).reshape(k // 32, 32, n)
    amax = np.abs(w).max(1)
    byte = np.clip(np.where(amax > 0, np.frexp(amax)[1] - 1 + 127 - 7, 1), 1, 254)
    scaled = (w * np.exp2(127.0 - byte)[:, None, :]).reshape(k, n).astype(np.float32)
    words = np.ascontiguousarray(scaled.reshape(k // 512, 128, 4, n).transpose(0, 1, 3, 2)).astype(ml_dtypes.float8_e4m3fn).view(np.uint8)
    return words, np.ascontiguousarray(byte.astype(np.uint8).reshape(k // 512, 16, n))


def unpack_weight(words, scales):
    g, p, n, _ = words.shape
    vals = np.ascontiguousarray(words).view(ml_dtypes.float8_e4m3fn).astype(np.float64) * np.repeat(np.exp2(scales.astype(np.float64) - 127.0), 8, axis=1)[..., None]
    return vals.transpose(0, 1, 3, 2).reshape(g * 512, n)


K, T, E, C, N = 1536, 1024, 8, 256, 128


def by_expert(wq, xq):
    return np.concatenate([wq[e].T @ xq[:, e * C:(e + 1) * C] for e in range(E)], axis=1)


def setup_inputs():
    n = np.random.standard_normal
    s = mx_kscale(K)[:, None]
    first = np.random.permutation(np.repeat(np.arange(E), T // E))
    second = (first + 1 + np.random.permutation(np.repeat(np.arange(E - 1), -(-T // (E - 1)))[:T])) % E
    while np.bincount(second, minlength=E).max() != T // E:
        load = np.bincount(second, minlength=E); hi, lo = int(load.argmax()), int(load.argmin())
        t = np.flatnonzero((second == hi) & (first != lo))[0]; second[t] = lo
    slot_token = np.empty(E * C, np.int64); pos = np.empty((2, T), np.int64); fill = np.zeros(E, np.int64)
    place = np.stack([np.random.permutation(C) for _ in range(E)])
    for r, deal in enumerate((first, second)):
        for t in np.random.permutation(T):
            e = deal[t]; j = e * C + place[e, fill[e]]; fill[e] += 1; slot_token[j] = t; pos[r, t] = j
    g = np.random.uniform(0.2, 0.8, T)
    packed = [pack_weight(m) for m in n((E, K, N)) / np.sqrt(K) / s[None]]
    return {
        "xT": (n((K, T)) * s).astype(np.float32),
        "w_words": np.stack([m[0] for m in packed]),
        "w_scales": np.stack([m[1] for m in packed]),
        "gate": np.stack([np.tile(g, (N, 1)), np.tile(1.0 - g, (N, 1))]).astype(np.float32),
        "offs": striped(slot_token),
        "pos1": striped(pos[0]),
        "pos2": striped(pos[1]),
    }


def reference(xT, w_words, w_scales, gate, offs, pos1, pos2):
    idx = unstriped(offs)
    xq = mxq(f64(xT)[:, idx], 0, "e4m3")
    w = np.stack([unpack_weight(w_words[e], w_scales[e]) for e in range(E)])
    y = by_expert(w, xq)
    return f64(gate[0]) * y[:, unstriped(pos1)] + f64(gate[1]) * y[:, unstriped(pos2)]

@@ -1,0 +1,142 @@
+from contextlib import ExitStack
+
+import concourse.mybir as mybir
+
+K, T, E, C, N = 1536, 1024, 8, 256, 128
+P = 128
+PACK = 4
+PASSES = K // (P * PACK)
+SLOTS = E * C
+FLOPS = 2 * K * N * SLOTS
+
+F32 = mybir.dt.float32
+BF16 = mybir.dt.bfloat16
+I32 = mybir.dt.int32
+U32 = mybir.dt.uint32
+U16 = mybir.dt.uint16
+U8 = mybir.dt.uint8
+FP8X4 = mybir.dt.float8_e4m3fn_x4
+MULT = mybir.AluOpType.mult
+
+CHUNKS = ((512, 256, 256), (512, 512), (512, 256, 256))
+VECTOR_SHARE = ((320, 160, 160), (0, 0), (0, 0, 0))
+EARLY = (768, 768, 512)
+LATE = (512, 512, 512, 256, 256)
+
+
+def tile_routed_moe_kernel(tc, xT, w_words, w_scales, gate, offs, pos1, pos2, out):
+    nc = tc.nc
+    with ExitStack() as ctx:
+        keep = ctx.enter_context(tc.tile_pool(name="keep", bufs=1))
+        psum = ctx.enter_context(tc.psum_pool(name="psum", bufs=1))
+
+        offs_sb = keep.tile([P, SLOTS // 16], U16, name="offs_sb")
+        pos1_sb = keep.tile([P, T // 16], U16, name="pos1_sb")
+        pos2_sb = keep.tile([P, T // 16], U16, name="pos2_sb")
+        tok_scales = keep.tile([P, T], U8, name="tok_scales", align_bytes=64)
+        nc.gpsimd.memset(tok_scales[:], 0)
+        w_sc = keep.tile([P, E * PASSES, N], U8, name="w_sc", align_bytes=64)
+        nc.vector.memset(w_sc[:].rearrange("p g n -> p (g n)").bitcast(I32), 0)
+
+        x_view = xT.rearrange("(a p r) t -> a p r t", p=P, r=PACK)
+        raws = []
+        for a in range(PASSES):
+            start = 0
+            for c, width in enumerate(CHUNKS[a]):
+                raw = keep.tile([P, PACK, width], F32, name=f"raw{a}_{c}")
+                nc.sync.dma_start(out=raw[:], in_=x_view[a, :, :, start : start + width])
+                raws.append(raw)
+                start += width
+            if a == 0:
+                nc.sync.dma_start(offs_sb[:], offs)
+
+        w_sb = keep.tile([P, E * PASSES, N], U32, name="w_sb", align_bytes=64)
+        for q in range(4):
+            nc.sync.dma_start(
+                out=w_sc[32 * q : 32 * q + 4, :, :].bitcast(I32),
+                in_=w_scales.rearrange("e a (q r) n -> q r (e a) n", r=4)[q].bitcast(I32),
+            )
+        w_view = w_words.rearrange("e a p n r -> p (e a) (n r)")
+        for h in range(2):
+            g = slice(h * 12, (h + 1) * 12)
+            nc.sync.dma_start(out=w_sb[:, g, :].bitcast(I32), in_=w_view[:, g, :].bitcast(I32))
+        nc.sync.dma_start(pos1_sb[:], pos1)
+        nc.sync.dma_start(pos2_sb[:], pos2)
+        gates = []
+        for i in range(2):
+            g_sb = keep.tile([P, T], F32, name=f"gate{i}")
+            nc.sync.dma_start(out=g_sb[:], in_=gate[i])
+            gates.append(g_sb)
+
+        slot_scales = keep.tile([P, SLOTS], U8, name="slot_scales", align_bytes=64)
+        slot_words = [keep.tile([P, SLOTS], U32, name=f"slot_words{a}", align_bytes=64) for a in range(PASSES)]
+        tok_words = [keep.tile([P, T], U32, name=f"tok_words{a}", align_bytes=64) for a in range(PASSES)]
+
+        def gather(dst, window, start, width):
+            nc.vector.tensor_copy(
+                dst[:, start : start + width],
+                window[:].indirect(offs_sb[:, start // 16 : (start + width) // 16]),
+            )
+
+        i = 0
+        for a in range(PASSES):
+            start = 0
+            for c, width in enumerate(CHUNKS[a]):
+                raw = raws[i]
+                i += 1
+                grouped = keep.tile([P, width, PACK], BF16, name=f"grouped{a}_{c}", align_bytes=64)
+                vw = VECTOR_SHARE[a][c]
+                if vw:
+                    nc.vector.tensor_copy(out=grouped[:, :vw, :], in_=raw[:, :, :vw].rearrange("p r t -> p t r"))
+                nc.scalar.copy(out=grouped[:, vw:, :], in_=raw[:, :, vw:].rearrange("p r t -> p t r"))
+                cols = slice(start, start + width)
+                nc.vector.quantize_mx(
+                    out=tok_words[a][:, cols].bitcast(FP8X4),
+                    scales=tok_scales[4 * a : P, cols],
+                    in_=grouped[:].rearrange("p t r -> p (t r)"),
+                )
+                start += width
+            if a < PASSES - 1:
+                start = 0
+                for width in EARLY:
+                    gather(slot_words[a], tok_words[a], start, width)
+                    start += width
+
+        start = 0
+        for width in EARLY:
+            gather(slot_scales, tok_scales, start, width)
+            start += width
+        start = 0
+        for width in LATE:
+            gather(slot_words[PASSES - 1], tok_words[PASSES - 1], start, width)
+            start += width
+
+        y = keep.tile([P, SLOTS], F32, name="y")
+        for e in range(E):
+            cols = slice(e * C, (e + 1) * C)
+            acc = psum.tile([N, C], F32, name=f"acc{e}")
+            for a in range(PASSES):
+                nc.tensor.matmul_mx(
+                    out=acc[:],
+                    lhsT=w_sb[:, e * PASSES + a, :].bitcast(FP8X4),
+                    lhsT_scale=w_sc[:, e * PASSES + a, :],
+                    rhs=slot_words[a][:, cols].bitcast(FP8X4),
+                    rhs_scale=slot_scales[4 * a : P, cols],
+                    start=(a == 0),
+                    stop=(a == PASSES - 1),
+                )
+            nc.scalar.copy(out=y[:, cols], in_=acc[:])
+
+        first = keep.tile([P, T], F32, name="first")
+        second = keep.tile([P, T], F32, name="second")
+        total = keep.tile([P, T], F32, name="total")
+        nc.vector.tensor_tensor(first[:], y[:].indirect(pos1_sb[:]), gates[0][:], MULT)
+        start = 0
+        for width in (512, 256, 256):
+            cols = slice(start, start + width)
+            nc.vector.tensor_tensor(
+                second[:, cols], y[:].indirect(pos2_sb[:, start // 16 : (start + width) // 16]), gates[1][:, cols], MULT
+            )
+            nc.vector.tensor_add(total[:, cols], first[:, cols], second[:, cols])
+            nc.sync.dma_start(out=out[:, cols], in_=total[:, cols])
+            start += width

@@ -18,10 +18,12 @@ U8 = mybir.dt.uint8
 FP8X4 = mybir.dt.float8_e4m3fn_x4
 MULT = mybir.AluOpType.mult
 
-CHUNKS = ((512, 256, 256), (512, 512), (512, 256, 256))
-VECTOR_SHARE = ((320, 160, 160), (0, 0), (0, 0, 0))
+CHUNKS = (384, 384, 256)
+VECTOR_SHARE = ((240, 240, 160), (0, 0, 160), (0, 0, 128))
+QUANTS = (256, 512, 256)
 EARLY = (768, 768, 512)
-LATE = (512, 512, 512, 256, 256)
+LATE = (512, 512, 512, 256, 128, 128)
+GROUPS = tuple((e, e * C, C) for e in range(E - 1)) + ((E - 1, (E - 1) * C, C // 2), (E - 1, (E - 1) * C + C // 2, C // 2))
 
 
 def tile_routed_moe_kernel(tc, xT, w_words, w_scales, gate, offs, pos1, pos2, out):
@@ -42,7 +44,7 @@ def tile_routed_moe_kernel(tc, xT, w_words, w_scales, gate, offs, pos1, pos2, ou
         raws = []
         for a in range(PASSES):
             start = 0
-            for c, width in enumerate(CHUNKS[a]):
+            for c, width in enumerate(CHUNKS):
                 raw = keep.tile([P, PACK, width], F32, name=f"raw{a}_{c}")
                 nc.sync.dma_start(out=raw[:], in_=x_view[a, :, :, start : start + width])
                 raws.append(raw)
@@ -81,21 +83,29 @@ def tile_routed_moe_kernel(tc, xT, w_words, w_scales, gate, offs, pos1, pos2, ou
         i = 0
         for a in range(PASSES):
             start = 0
-            for c, width in enumerate(CHUNKS[a]):
+            grouped = keep.tile([P, T, PACK], BF16, name=f"grouped{a}", align_bytes=64)
+            quants = list(QUANTS)
+            done = 0
+            for c, width in enumerate(CHUNKS):
                 raw = raws[i]
                 i += 1
-                grouped = keep.tile([P, width, PACK], BF16, name=f"grouped{a}_{c}", align_bytes=64)
                 vw = VECTOR_SHARE[a][c]
+                mid = start + vw
+                end = start + width
                 if vw:
-                    nc.vector.tensor_copy(out=grouped[:, :vw, :], in_=raw[:, :, :vw].rearrange("p r t -> p t r"))
-                nc.scalar.copy(out=grouped[:, vw:, :], in_=raw[:, :, vw:].rearrange("p r t -> p t r"))
-                cols = slice(start, start + width)
-                nc.vector.quantize_mx(
-                    out=tok_words[a][:, cols].bitcast(FP8X4),
-                    scales=tok_scales[4 * a : P, cols],
-                    in_=grouped[:].rearrange("p t r -> p (t r)"),
-                )
-                start += width
+                    nc.vector.tensor_copy(out=grouped[:, start:mid, :], in_=raw[:, :, :vw].rearrange("p r t -> p t r"))
+                if vw < width:
+                    nc.scalar.copy(out=grouped[:, mid:end, :], in_=raw[:, :, vw:].rearrange("p r t -> p t r"))
+                start = end
+                while quants and done + quants[0] <= end:
+                    cols = slice(done, done + quants[0])
+                    nc.vector.quantize_mx(
+                        out=tok_words[a][:, cols].bitcast(FP8X4),
+                        scales=tok_scales[4 * a : P, cols],
+                        in_=grouped[:, cols, :].rearrange("p t r -> p (t r)"),
+                    )
+                    done += quants[0]
+                    quants = quants[1:]
             if a < PASSES - 1:
                 start = 0
                 for width in EARLY:
@@ -112,9 +122,9 @@ def tile_routed_moe_kernel(tc, xT, w_words, w_scales, gate, offs, pos1, pos2, ou
             start += width
 
         y = keep.tile([P, SLOTS], F32, name="y")
-        for e in range(E):
-            cols = slice(e * C, (e + 1) * C)
-            acc = psum.tile([N, C], F32, name=f"acc{e}")
+        for g, (e, first_slot, width) in enumerate(GROUPS):
+            cols = slice(first_slot, first_slot + width)
+            acc = psum.tile([N, width], F32, name=f"acc{g % 8}")
             for a in range(PASSES):
                 nc.tensor.matmul_mx(
                     out=acc[:],
@@ -125,7 +135,10 @@ def tile_routed_moe_kernel(tc, xT, w_words, w_scales, gate, offs, pos1, pos2, ou
                     start=(a == 0),
                     stop=(a == PASSES - 1),
                 )
-            nc.scalar.copy(out=y[:, cols], in_=acc[:])
+            if g == len(GROUPS) - 1:
+                nc.vector.tensor_copy(out=y[:, cols], in_=acc[:])
+            else:
+                nc.scalar.copy(out=y[:, cols], in_=acc[:])
 
         first = keep.tile([P, T], F32, name="first")
         second = keep.tile([P, T], F32, name="second")

@@ -18,9 +18,9 @@ U8 = mybir.dt.uint8
 FP8X4 = mybir.dt.float8_e4m3fn_x4
 MULT = mybir.AluOpType.mult
 
-CHUNKS = (384, 384, 256)
-VECTOR_SHARE = ((240, 240, 160), (0, 0, 160), (0, 0, 128))
-QUANTS = (256, 512, 256)
+CHUNKS = (512, 256, 256)
+VECTOR_SHARE = ((320, 160, 160), (0, 0, 192), (0, 0, 128))
+QUANTS = (512, 256, 256)
 EARLY = (768, 768, 512)
 LATE = (512, 512, 512, 256, 128, 128)
 GROUPS = tuple((e, e * C, C) for e in range(E - 1)) + ((E - 1, (E - 1) * C, C // 2), (E - 1, (E - 1) * C + C // 2, C // 2))
@@ -59,8 +59,8 @@ def tile_routed_moe_kernel(tc, xT, w_words, w_scales, gate, offs, pos1, pos2, ou
                 in_=w_scales.rearrange("e a (q r) n -> q r (e a) n", r=4)[q].bitcast(I32),
             )
         w_view = w_words.rearrange("e a p n r -> p (e a) (n r)")
-        for h in range(2):
-            g = slice(h * 12, (h + 1) * 12)
+        for h in range(4):
+            g = slice(h * 6, (h + 1) * 6)
             nc.sync.dma_start(out=w_sb[:, g, :].bitcast(I32), in_=w_view[:, g, :].bitcast(I32))
         nc.sync.dma_start(pos1_sb[:], pos1)
         nc.sync.dma_start(pos2_sb[:], pos2)
@@ -93,9 +93,15 @@ def tile_routed_moe_kernel(tc, xT, w_words, w_scales, gate, offs, pos1, pos2, ou
                 mid = start + vw
                 end = start + width
                 if vw:
-                    nc.vector.tensor_copy(out=grouped[:, start:mid, :], in_=raw[:, :, :vw].rearrange("p r t -> p t r"))
+                    nc.vector.tensor_copy(
+                        out=grouped[:, start:mid, :].rearrange("p (c i) r -> p c r i", i=4),
+                        in_=raw[:, :, :vw].rearrange("p r (c i) -> p c r i", i=4),
+                    )
                 if vw < width:
-                    nc.scalar.copy(out=grouped[:, mid:end, :], in_=raw[:, :, vw:].rearrange("p r t -> p t r"))
+                    nc.scalar.copy(
+                        out=grouped[:, mid:end, :].rearrange("p (c i) r -> p c r i", i=4),
+                        in_=raw[:, :, vw:].rearrange("p r (c i) -> p c r i", i=4),
+                    )
                 start = end
                 while quants and done + quants[0] <= end:
                     cols = slice(done, done + quants[0])
@@ -122,23 +128,36 @@ def tile_routed_moe_kernel(tc, xT, w_words, w_scales, gate, offs, pos1, pos2, ou
             start += width
 
         y = keep.tile([P, SLOTS], F32, name="y")
+        accs = {}
+
+        def multiply(g, a):
+            e, first_slot, width = GROUPS[g]
+            cols = slice(first_slot, first_slot + width)
+            if a == 0:
+                accs[g] = psum.tile([N, width], F32, name=f"acc{g % 8}")
+            nc.tensor.matmul_mx(
+                out=accs[g][:],
+                lhsT=w_sb[:, e * PASSES + a, :].bitcast(FP8X4),
+                lhsT_scale=w_sc[:, e * PASSES + a, :],
+                rhs=slot_words[a][:, cols].bitcast(FP8X4),
+                rhs_scale=slot_scales[4 * a : P, cols],
+                start=(a == 0),
+                stop=(a == PASSES - 1),
+            )
+
+        for g in range(8):
+            multiply(g, 0)
+            multiply(g, 1)
         for g, (e, first_slot, width) in enumerate(GROUPS):
             cols = slice(first_slot, first_slot + width)
-            acc = psum.tile([N, width], F32, name=f"acc{g % 8}")
-            for a in range(PASSES):
-                nc.tensor.matmul_mx(
-                    out=acc[:],
-                    lhsT=w_sb[:, e * PASSES + a, :].bitcast(FP8X4),
-                    lhsT_scale=w_sc[:, e * PASSES + a, :],
-                    rhs=slot_words[a][:, cols].bitcast(FP8X4),
-                    rhs_scale=slot_scales[4 * a : P, cols],
-                    start=(a == 0),
-                    stop=(a == PASSES - 1),
-                )
+            multiply(g, 2)
             if g == len(GROUPS) - 1:
-                nc.vector.tensor_copy(out=y[:, cols], in_=acc[:])
+                nc.vector.tensor_copy(out=y[:, cols], in_=accs[g][:])
             else:
-                nc.scalar.copy(out=y[:, cols], in_=acc[:])
+                nc.scalar.copy(out=y[:, cols], in_=accs[g][:])
+            if g == 0:
+                multiply(8, 0)
+                multiply(8, 1)
 
         first = keep.tile([P, T], F32, name="first")
         second = keep.tile([P, T], F32, name="second")

@@ -21,8 +21,9 @@ MULT = mybir.AluOpType.mult
 CHUNKS = (512, 256, 256)
 VECTOR_SHARE = ((320, 160, 160), (0, 0, 192), (0, 0, 128))
 QUANTS = (512, 256, 256)
-EARLY = (768, 768, 512)
+EARLY = (512, 1536)
 LATE = (512, 512, 512, 256, 128, 128)
+WINDOW = 2 * T
 GROUPS = tuple((e, e * C, C) for e in range(E - 1)) + ((E - 1, (E - 1) * C, C // 2), (E - 1, (E - 1) * C + C // 2, C // 2))
 
 
@@ -35,11 +36,13 @@ def tile_routed_moe_kernel(tc, xT, w_words, w_scales, gate, offs, pos1, pos2, ou
         offs_sb = keep.tile([P, SLOTS // 16], U16, name="offs_sb")
         pos1_sb = keep.tile([P, T // 16], U16, name="pos1_sb")
         pos2_sb = keep.tile([P, T // 16], U16, name="pos2_sb")
-        tok_scales = keep.tile([P, T], U8, name="tok_scales", align_bytes=64)
+        tok_scales = keep.tile([P, WINDOW], U8, name="tok_scales", align_bytes=64)
         nc.gpsimd.memset(tok_scales[:], 0)
         w_sc = keep.tile([P, E * PASSES, N], U8, name="w_sc", align_bytes=64)
         nc.vector.memset(w_sc[:].rearrange("p g n -> p (g n)").bitcast(I32), 0)
 
+        all_words = keep.tile([P, (PASSES + 1) * T], I32, name="all_words", align_bytes=64)
+        nc.vector.memset(all_words[:, PASSES * T :], 0)
         x_view = xT.rearrange("(a p r) t -> a p r t", p=P, r=PACK)
         raws = []
         for a in range(PASSES):
@@ -48,9 +51,9 @@ def tile_routed_moe_kernel(tc, xT, w_words, w_scales, gate, offs, pos1, pos2, ou
                 raw = keep.tile([P, PACK, width], F32, name=f"raw{a}_{c}")
                 nc.sync.dma_start(out=raw[:], in_=x_view[a, :, :, start : start + width])
                 raws.append(raw)
+                if a == 0 and c == 0:
+                    nc.sync.dma_start(offs_sb[:], offs)
                 start += width
-            if a == 0:
-                nc.sync.dma_start(offs_sb[:], offs)
 
         w_sb = keep.tile([P, E * PASSES, N], U32, name="w_sb", align_bytes=64)
         for q in range(4):
@@ -72,12 +75,12 @@ def tile_routed_moe_kernel(tc, xT, w_words, w_scales, gate, offs, pos1, pos2, ou
 
         slot_scales = keep.tile([P, SLOTS], U8, name="slot_scales", align_bytes=64)
         slot_words = [keep.tile([P, SLOTS], U32, name=f"slot_words{a}", align_bytes=64) for a in range(PASSES)]
-        tok_words = [keep.tile([P, T], U32, name=f"tok_words{a}", align_bytes=64) for a in range(PASSES)]
+        tok_words = [all_words[:, (PASSES - 1 - a) * T : (PASSES + 1 - a) * T].bitcast(U32) for a in range(PASSES)]
 
         def gather(dst, window, start, width):
             nc.vector.tensor_copy(
                 dst[:, start : start + width],
-                window[:].indirect(offs_sb[:, start // 16 : (start + width) // 16]),
+                window.indirect(offs_sb[:, start // 16 : (start + width) // 16]),
             )
 
         i = 0
@@ -120,11 +123,11 @@ def tile_routed_moe_kernel(tc, xT, w_words, w_scales, gate, offs, pos1, pos2, ou
 
         start = 0
         for width in EARLY:
-            gather(slot_scales, tok_scales, start, width)
+            gather(slot_scales, tok_scales[:], start, width)
             start += width
         start = 0
         for width in LATE:
-            gather(slot_words[PASSES - 1], tok_words[PASSES - 1], start, width)
+            gather(slot_words[PASSES - 1], tok_words[PASSES - 1][:, :T], start, width)
             start += width
 
         y = keep.tile([P, SLOTS], F32, name="y")
@@ -151,7 +154,7 @@ def tile_routed_moe_kernel(tc, xT, w_words, w_scales, gate, offs, pos1, pos2, ou
         for g, (e, first_slot, width) in enumerate(GROUPS):
             cols = slice(first_slot, first_slot + width)
             multiply(g, 2)
-            if g == len(GROUPS) - 1:
+            if g >= E - 1:
                 nc.vector.tensor_copy(out=y[:, cols], in_=accs[g][:])
             else:
                 nc.scalar.copy(out=y[:, cols], in_=accs[g][:])
@@ -164,7 +167,7 @@ def tile_routed_moe_kernel(tc, xT, w_words, w_scales, gate, offs, pos1, pos2, ou
         total = keep.tile([P, T], F32, name="total")
         nc.vector.tensor_tensor(first[:], y[:].indirect(pos1_sb[:]), gates[0][:], MULT)
         start = 0
-        for width in (512, 256, 256):
+        for width in (512, 384, 128):
             cols = slice(start, start + width)
             nc.vector.tensor_tensor(
                 second[:, cols], y[:].indirect(pos2_sb[:, start // 16 : (start + width) // 16]), gates[1][:, cols], MULT

@@ -19,12 +19,13 @@ FP8X4 = mybir.dt.float8_e4m3fn_x4
 MULT = mybir.AluOpType.mult
 
 CHUNKS = (512, 256, 256)
-VECTOR_SHARE = ((320, 160, 160), (0, 0, 192), (0, 0, 128))
+VECTOR_SHARE = ((320, 160, 160), (0, 0, 128), (0, 0, 0))
+GPSIMD_SHARE = ((0, 0, 0), (128, 0, 0), (192, 0, 0))
 QUANTS = (512, 256, 256)
 EARLY = (512, 1536)
-LATE = (512, 512, 512, 256, 128, 128)
+LATE = (512, 512, 512, 256, 256)
 WINDOW = 2 * T
-GROUPS = tuple((e, e * C, C) for e in range(E - 1)) + ((E - 1, (E - 1) * C, C // 2), (E - 1, (E - 1) * C + C // 2, C // 2))
+GROUPS = tuple((e, e * C, C) for e in range(E))
 
 
 def tile_routed_moe_kernel(tc, xT, w_words, w_scales, gate, offs, pos1, pos2, out):
@@ -93,17 +94,20 @@ def tile_routed_moe_kernel(tc, xT, w_words, w_scales, gate, offs, pos1, pos2, ou
                 raw = raws[i]
                 i += 1
                 vw = VECTOR_SHARE[a][c]
-                mid = start + vw
+                gw = GPSIMD_SHARE[a][c]
+                mid = start + vw + gw
+                if gw:
+                    nc.gpsimd.tensor_copy(out=grouped[:, start + vw : mid, :], in_=raw[:, :, vw : vw + gw].rearrange("p r t -> p t r"))
                 end = start + width
                 if vw:
                     nc.vector.tensor_copy(
-                        out=grouped[:, start:mid, :].rearrange("p (c i) r -> p c r i", i=4),
+                        out=grouped[:, start : start + vw, :].rearrange("p (c i) r -> p c r i", i=4),
                         in_=raw[:, :, :vw].rearrange("p r (c i) -> p c r i", i=4),
                     )
-                if vw < width:
+                if vw + gw < width:
                     nc.scalar.copy(
                         out=grouped[:, mid:end, :].rearrange("p (c i) r -> p c r i", i=4),
-                        in_=raw[:, :, vw:].rearrange("p r (c i) -> p c r i", i=4),
+                        in_=raw[:, :, vw + gw :].rearrange("p r (c i) -> p c r i", i=4),
                     )
                 start = end
                 while quants and done + quants[0] <= end:
@@ -122,7 +126,7 @@ def tile_routed_moe_kernel(tc, xT, w_words, w_scales, gate, offs, pos1, pos2, ou
                     start += width
 
         start = 0
-        for width in EARLY:
+        for width in (1024, 1024):
             gather(slot_scales, tok_scales[:], start, width)
             start += width
         start = 0
@@ -148,19 +152,25 @@ def tile_routed_moe_kernel(tc, xT, w_words, w_scales, gate, offs, pos1, pos2, ou
                 stop=(a == PASSES - 1),
             )
 
-        for g in range(8):
-            multiply(g, 0)
-            multiply(g, 1)
-        for g, (e, first_slot, width) in enumerate(GROUPS):
+        def finish(g):
+            e, first_slot, width = GROUPS[g]
             cols = slice(first_slot, first_slot + width)
             multiply(g, 2)
-            if g >= E - 1:
+            if g == E - 1:
                 nc.vector.tensor_copy(out=y[:, cols], in_=accs[g][:])
             else:
                 nc.scalar.copy(out=y[:, cols], in_=accs[g][:])
-            if g == 0:
-                multiply(8, 0)
-                multiply(8, 1)
+
+        ahead = 6
+        for g in range(ahead):
+            multiply(g, 0)
+            multiply(g, 1)
+        for g in range(E):
+            finish(g)
+            if g % 2 == 1 and ahead < E:
+                multiply(ahead, 0)
+                multiply(ahead, 1)
+                ahead += 1
 
         first = keep.tile([P, T], F32, name="first")
         second = keep.tile([P, T], F32, name="second")

from contextlib import ExitStack

import concourse.mybir as mybir

K, T, E, C, N = 1536, 1024, 8, 256, 128
P = 128
PACK = 4
PASSES = K // (P * PACK)
SLOTS = E * C
FLOPS = 2 * K * N * SLOTS

F32 = mybir.dt.float32
BF16 = mybir.dt.bfloat16
I32 = mybir.dt.int32
U32 = mybir.dt.uint32
U16 = mybir.dt.uint16
U8 = mybir.dt.uint8
FP8X4 = mybir.dt.float8_e4m3fn_x4
MULT = mybir.AluOpType.mult

CHUNKS = (512, 256, 256)
VECTOR_SHARE = ((320, 160, 160), (0, 0, 128), (0, 0, 0))
GPSIMD_SHARE = ((0, 0, 0), (128, 0, 0), (192, 0, 0))
QUANTS = (512, 256, 256)
EARLY = (512, 1536)
LATE = (512, 512, 512, 256, 256)
WINDOW = 2 * T
GROUPS = tuple((e, e * C, C) for e in range(E))


def tile_routed_moe_kernel(tc, xT, w_words, w_scales, gate, offs, pos1, pos2, out):
    nc = tc.nc
    with ExitStack() as ctx:
        keep = ctx.enter_context(tc.tile_pool(name="keep", bufs=1))
        psum = ctx.enter_context(tc.psum_pool(name="psum", bufs=1))

        offs_sb = keep.tile([P, SLOTS // 16], U16, name="offs_sb")
        pos1_sb = keep.tile([P, T // 16], U16, name="pos1_sb")
        pos2_sb = keep.tile([P, T // 16], U16, name="pos2_sb")
        tok_scales = keep.tile([P, WINDOW], U8, name="tok_scales", align_bytes=64)
        nc.gpsimd.memset(tok_scales[:], 0)
        w_sc = keep.tile([P, E * PASSES, N], U8, name="w_sc", align_bytes=64)
        nc.vector.memset(w_sc[:].rearrange("p g n -> p (g n)").bitcast(I32), 0)

        all_words = keep.tile([P, (PASSES + 1) * T], I32, name="all_words", align_bytes=64)
        nc.vector.memset(all_words[:, PASSES * T :], 0)
        x_view = xT.rearrange("(a p r) t -> a p r t", p=P, r=PACK)
        raws = []
        for a in range(PASSES):
            start = 0
            for c, width in enumerate(CHUNKS):
                raw = keep.tile([P, PACK, width], F32, name=f"raw{a}_{c}")
                nc.sync.dma_start(out=raw[:], in_=x_view[a, :, :, start : start + width])
                raws.append(raw)
                if a == 0 and c == 0:
                    nc.sync.dma_start(offs_sb[:], offs)
                start += width

        w_sb = keep.tile([P, E * PASSES, N], U32, name="w_sb", align_bytes=64)
        for q in range(4):
            nc.sync.dma_start(
                out=w_sc[32 * q : 32 * q + 4, :, :].bitcast(I32),
                in_=w_scales.rearrange("e a (q r) n -> q r (e a) n", r=4)[q].bitcast(I32),
            )
        w_view = w_words.rearrange("e a p n r -> p (e a) (n r)")
        for h in range(4):
            g = slice(h * 6, (h + 1) * 6)
            nc.sync.dma_start(out=w_sb[:, g, :].bitcast(I32), in_=w_view[:, g, :].bitcast(I32))
        nc.sync.dma_start(pos1_sb[:], pos1)
        nc.sync.dma_start(pos2_sb[:], pos2)
        gates = []
        for i in range(2):
            g_sb = keep.tile([P, T], F32, name=f"gate{i}")
            nc.sync.dma_start(out=g_sb[:], in_=gate[i])
            gates.append(g_sb)

        slot_scales = keep.tile([P, SLOTS], U8, name="slot_scales", align_bytes=64)
        slot_words = [keep.tile([P, SLOTS], U32, name=f"slot_words{a}", align_bytes=64) for a in range(PASSES)]
        tok_words = [all_words[:, (PASSES - 1 - a) * T : (PASSES + 1 - a) * T].bitcast(U32) for a in range(PASSES)]

        def gather(dst, window, start, width):
            nc.vector.tensor_copy(
                dst[:, start : start + width],
                window.indirect(offs_sb[:, start // 16 : (start + width) // 16]),
            )

        i = 0
        for a in range(PASSES):
            start = 0
            grouped = keep.tile([P, T, PACK], BF16, name=f"grouped{a}", align_bytes=64)
            quants = list(QUANTS)
            done = 0
            for c, width in enumerate(CHUNKS):
                raw = raws[i]
                i += 1
                vw = VECTOR_SHARE[a][c]
                gw = GPSIMD_SHARE[a][c]
                mid = start + vw + gw
                if gw:
                    nc.gpsimd.tensor_copy(out=grouped[:, start + vw : mid, :], in_=raw[:, :, vw : vw + gw].rearrange("p r t -> p t r"))
                end = start + width
                if vw:
                    nc.vector.tensor_copy(
                        out=grouped[:, start : start + vw, :].rearrange("p (c i) r -> p c r i", i=4),
                        in_=raw[:, :, :vw].rearrange("p r (c i) -> p c r i", i=4),
                    )
                if vw + gw < width:
                    nc.scalar.copy(
                        out=grouped[:, mid:end, :].rearrange("p (c i) r -> p c r i", i=4),
                        in_=raw[:, :, vw + gw :].rearrange("p r (c i) -> p c r i", i=4),
                    )
                start = end
                while quants and done + quants[0] <= end:
                    cols = slice(done, done + quants[0])
                    nc.vector.quantize_mx(
                        out=tok_words[a][:, cols].bitcast(FP8X4),
                        scales=tok_scales[4 * a : P, cols],
                        in_=grouped[:, cols, :].rearrange("p t r -> p (t r)"),
                    )
                    done += quants[0]
                    quants = quants[1:]
            if a < PASSES - 1:
                start = 0
                for width in EARLY:
                    gather(slot_words[a], tok_words[a], start, width)
                    start += width

        start = 0
        for width in (1024, 1024):
            gather(slot_scales, tok_scales[:], start, width)
            start += width
        start = 0
        for width in LATE:
            gather(slot_words[PASSES - 1], tok_words[PASSES - 1][:, :T], start, width)
            start += width

        y = keep.tile([P, SLOTS], F32, name="y")
        accs = {}

        def multiply(g, a):
            e, first_slot, width = GROUPS[g]
            cols = slice(first_slot, first_slot + width)
            if a == 0:
                accs[g] = psum.tile([N, width], F32, name=f"acc{g % 8}")
            nc.tensor.matmul_mx(
                out=accs[g][:],
                lhsT=w_sb[:, e * PASSES + a, :].bitcast(FP8X4),
                lhsT_scale=w_sc[:, e * PASSES + a, :],
                rhs=slot_words[a][:, cols].bitcast(FP8X4),
                rhs_scale=slot_scales[4 * a : P, cols],
                start=(a == 0),
                stop=(a == PASSES - 1),
            )

        def finish(g):
            e, first_slot, width = GROUPS[g]
            cols = slice(first_slot, first_slot + width)
            multiply(g, 2)
            if g == E - 1:
                nc.vector.tensor_copy(out=y[:, cols], in_=accs[g][:])
            else:
                nc.scalar.copy(out=y[:, cols], in_=accs[g][:])

        ahead = 6
        for g in range(ahead):
            multiply(g, 0)
            multiply(g, 1)
        for g in range(E):
            finish(g)
            if g % 2 == 1 and ahead < E:
                multiply(ahead, 0)
                multiply(ahead, 1)
                ahead += 1

        first = keep.tile([P, T], F32, name="first")
        second = keep.tile([P, T], F32, name="second")
        total = keep.tile([P, T], F32, name="total")
        nc.vector.tensor_tensor(first[:], y[:].indirect(pos1_sb[:]), gates[0][:], MULT)
        start = 0
        for width in (512, 384, 128):
            cols = slice(start, start + width)
            nc.vector.tensor_tensor(
                second[:, cols], y[:].indirect(pos2_sb[:, start // 16 : (start + width) // 16]), gates[1][:, cols], MULT
            )
            nc.vector.tensor_add(total[:, cols], first[:, cols], second[:, cols])
            nc.sync.dma_start(out=out[:, cols], in_=total[:, cols])
            start += width
